import numpy as np
import ml_dtypes


def mxq(x, axis, fmt="e4m3"):
    dtype, down = {"e4m3": (ml_dtypes.float8_e4m3fn, 7), "e5m2": (ml_dtypes.float8_e5m2, 14)}[fmt]
    v = np.moveaxis(np.asarray(x, np.float32).astype(ml_dtypes.bfloat16).astype(np.float64), axis, -1)
    blocks = v.reshape(v.shape[:-1] + (-1, 32))
    amax = np.abs(blocks).max(-1, keepdims=True)
    byte = np.maximum(np.where(amax > 0, np.frexp(amax)[1] - 1 + 127, 0) - down, 1)
    scale = np.exp2(byte - 127.0)
    codes = (blocks / scale).astype(np.float32).astype(dtype).astype(np.float64)
    return np.moveaxis((codes * scale).reshape(v.shape), -1, axis)


WIDE = False


def mx_kscale(k):
    if not WIDE:
        return np.ones(k)
    levels = np.array([10, -10, 5, -5, 0])
    if k % 512:
        return np.exp2(np.random.permutation(np.resize(levels, k // 32))).repeat(32)
    a = np.empty((k // 512, 16))
    for p in range(k // 512):
        a[p, :8] = np.random.permutation(np.resize(levels, 8))
        for g in range(8):
            far = levels[np.abs(levels - a[p, g]) >= 10]
            a[p, g + 8] = far[np.random.randint(len(far))]
    return np.exp2(a.ravel()).repeat(32)


def f64(x):
    return np.asarray(x).astype(np.float64)


def striped(idx):
    return np.tile(np.asarray(idx).reshape(-1, 16).T, (8, 1)).astype(np.uint16)


def unstriped(offs):
    return offs[:16].T.reshape(-1).astype(np.int64)


G, T, T2, D, M = 256, 1024, 1024, 1024, 256


def setup_inputs():
    n = np.random.standard_normal
    s = mx_kscale(D)[:, None]
    return {
        "xT": (n((D, T)) * s).astype(np.float32),
        "w": (n((D, M)) / np.sqrt(D) / s).astype(np.float32),
        "cache": n((M, T2)).astype(np.float32),
        "bias": (0.3 * n((M, 1))).astype(np.float32),
        "offs": striped(np.random.permutation(T)[:G]),
        "slots": striped(np.random.permutation(T2)[:G]),
    }


def reference(xT, w, cache, bias, offs, slots):
    y = mxq(f64(w), 0, "e4m3").T @ mxq(f64(xT)[:, unstriped(offs)], 0, "e4m3")
    y = y + f64(bias)
    out = f64(cache).copy()
    out[:, unstriped(slots)] = y
    return out

@@ -1,0 +1,137 @@
+from contextlib import ExitStack
+
+import concourse.mybir as mybir
+
+F32 = mybir.dt.float32
+BF16 = mybir.dt.bfloat16
+U32 = mybir.dt.uint32
+U16 = mybir.dt.uint16
+U8 = mybir.dt.uint8
+FP8X4 = mybir.dt.float8_e4m3fn_x4
+COPY = mybir.ActivationFunctionType.Copy
+IDENTITY = mybir.ActivationFunctionType.Identity
+
+P = 128
+PACK = 4
+G, T, T2, D, M = 256, 1024, 1024, 1024, 256
+PASSES = D // (P * PACK)
+BLOCKS = M // P
+
+FLOPS = 2 * D * M * G
+
+
+def tile_attend_fill_bias_kernel(tc, xT, w, cache, bias, offs, slots, out):
+    nc = tc.nc
+    x_rows = xT.rearrange("(g p j) n -> g p j n", p=P, j=PACK)
+    w_rows = w.rearrange("(g p j) m -> g p j m", p=P, j=PACK)
+    cache_rows = cache.rearrange("(p t) n -> t p n", t=BLOCKS)
+    out_rows = out.rearrange("(p t) n -> t p n", t=BLOCKS)
+
+    with ExitStack() as ctx:
+        lists = ctx.enter_context(tc.tile_pool(name="lists", bufs=1))
+        keep = ctx.enter_context(tc.tile_pool(name="keep", bufs=1))
+        psum = ctx.enter_context(tc.psum_pool(name="psum", bufs=1))
+
+        offs_sb = lists.tile([P, G // 16], U16, name="offs_sb")
+        nc.sync.dma_start(offs_sb[:], offs)
+        x_sb = {}
+        w_sb = []
+
+        def load_x(g, j0, count):
+            rows = keep.tile([P, count, T], F32, name=f"x_{g}_{j0}")
+            nc.sync.dma_start(out=rows[:], in_=x_rows[g, :, j0 : j0 + count, :])
+            for j in range(count):
+                x_sb[g, j0 + j] = rows[:, j, :]
+
+        def load_w(g):
+            rows = keep.tile([P, PACK, M], F32, name=f"w_{g}")
+            nc.sync.dma_start(out=rows[:], in_=w_rows[g])
+            w_sb.append(rows)
+
+        load_x(0, 0, 2)
+        load_x(0, 2, 2)
+        for j in range(PACK):
+            load_x(1, j, 1)
+        load_w(0)
+        load_w(1)
+        slots_sb = lists.tile([P, G // 16], U16, name="slots_sb")
+        nc.sync.dma_start(slots_sb[:], slots)
+        bias_sb = keep.tile([P, BLOCKS], F32, name="bias_sb")
+        nc.sync.dma_start(out=bias_sb[:], in_=bias.rearrange("(p t) o -> p (t o)", t=BLOCKS))
+        cache_sb = []
+        for t in range(BLOCKS):
+            rows = keep.tile([P, T2], F32, name=f"cache_{t}")
+            nc.sync.dma_start(out=rows[:], in_=cache_rows[t])
+            cache_sb.append(rows)
+
+        def quantize(name, grouped, width):
+            codes = keep.tile([P, width], U32, name=f"{name}_codes", align_bytes=64)
+            scales = keep.tile([P, width], U8, name=f"{name}_scales", align_bytes=64)
+            nc.vector.quantize_mx(
+                out=codes[:].bitcast(FP8X4),
+                scales=scales[:],
+                in_=grouped[:].rearrange("p n j -> p (n j)"),
+            )
+            return codes, scales
+
+        x_mx, w_mx = [], {}
+
+        def gather(g):
+            x_grouped = keep.tile([P, G, PACK], BF16, name=f"x_grouped_{g}", align_bytes=64)
+            for j in range(PACK):
+                nc.vector.tensor_copy(out=x_grouped[:, :, j], in_=x_sb[g, j].indirect(offs_sb[:]))
+            return x_grouped
+
+        def interleave(g, t, parts):
+            w_grouped = keep.tile([P, P, PACK], BF16, name=f"w_grouped_{g}_{t}", align_bytes=64)
+            source = w_sb[g][:].rearrange("p j (m t) -> p t m j", t=BLOCKS)[:, t]
+            for engine, m0, m1 in parts:
+                target = w_grouped[:, m0:m1, :].rearrange("p (c i) j -> p c j i", i=4)
+                rows = source[:, m0:m1, :].rearrange("p (c i) j -> p c j i", i=4)
+                if engine == "scalar":
+                    nc.scalar.activation(target, rows, COPY)
+                else:
+                    nc.vector.tensor_copy(out=target, in_=rows)
+            return w_grouped
+
+        pieces = [(0, 0, G // 2), (0, G // 2, G), (1, 0, G)]
+        acc = [psum.tile([P, n1 - n0], F32, name=f"acc_{t}_{n0}") for t, n0, n1 in pieces]
+
+        def multiply(g, t):
+            w_codes, w_scales = w_mx[g, t]
+            x_codes, x_scales = x_mx[g]
+            for i, (block, n0, n1) in enumerate(pieces):
+                if block == t:
+                    nc.tensor.matmul_mx(
+                        out=acc[i][:],
+                        lhsT=w_codes[:].bitcast(FP8X4),
+                        lhsT_scale=w_scales[:],
+                        rhs=x_codes[:, n0:n1].bitcast(FP8X4),
+                        rhs_scale=x_scales[:, n0:n1],
+                        start=(g == 0),
+                        stop=(g == PASSES - 1),
+                    )
+
+        x0 = gather(0)
+        x_mx.append(quantize("x0", x0, G))
+        x1 = gather(1)
+        x_mx.append(quantize("x1", x1, G))
+        wg = {}
+        for t in range(BLOCKS):
+            wg[0, t] = interleave(0, t, [("vector" if t == 0 else "scalar", 0, P)])
+        for t in range(BLOCKS):
+            w_mx[0, t] = quantize(f"w0{t}", wg[0, t], P)
+            multiply(0, t)
+        wg[1, 0] = interleave(1, 0, [("scalar", 0, P // 2), ("vector", P // 2, P)])
+        wg[1, 1] = interleave(1, 1, [("scalar", 0, P)])
+        for t in range(BLOCKS):
+            w_mx[1, t] = quantize(f"w1{t}", wg[1, t], P)
+            multiply(1, t)
+
+        for t in range(BLOCKS):
+            y = keep.tile([P, G], F32, name=f"y_{t}")
+            for i, (block, n0, n1) in enumerate(pieces):
+                if block == t:
+                    nc.scalar.activation(y[:, n0:n1], acc[i][:], IDENTITY, bias=bias_sb[:, t : t + 1])
+            nc.vector.tensor_copy(out=cache_sb[t][:].indirect(slots_sb[:]), in_=y[:])
+            nc.sync.dma_start(out=out_rows[t], in_=cache_sb[t][:])

@@ -1,6 +1,7 @@
 from contextlib import ExitStack
 
 import concourse.mybir as mybir
+from concourse.masks import make_identity
 
 F32 = mybir.dt.float32
 BF16 = mybir.dt.bfloat16
@@ -24,18 +25,15 @@ def tile_attend_fill_bias_kernel(tc, xT, w, cache, bias, offs, slots, out):
     nc = tc.nc
     x_rows = xT.rearrange("(g p j) n -> g p j n", p=P, j=PACK)
     w_rows = w.rearrange("(g p j) m -> g p j m", p=P, j=PACK)
-    cache_rows = cache.rearrange("(p t) n -> t p n", t=BLOCKS)
-    out_rows = out.rearrange("(p t) n -> t p n", t=BLOCKS)
+    cache_rows = cache.rearrange("(t p) n -> t p n", p=P)
+    out_rows = out.rearrange("(t p) n -> t p n", p=P)
 
     with ExitStack() as ctx:
         lists = ctx.enter_context(tc.tile_pool(name="lists", bufs=1))
         keep = ctx.enter_context(tc.tile_pool(name="keep", bufs=1))
         psum = ctx.enter_context(tc.psum_pool(name="psum", bufs=1))
 
-        offs_sb = lists.tile([P, G // 16], U16, name="offs_sb")
-        nc.sync.dma_start(offs_sb[:], offs)
         x_sb = {}
-        w_sb = []
 
         def load_x(g, j0, count):
             rows = keep.tile([P, count, T], F32, name=f"x_{g}_{j0}")
@@ -43,26 +41,40 @@ def tile_attend_fill_bias_kernel(tc, xT, w, cache, bias, offs, slots, out):
             for j in range(count):
                 x_sb[g, j0 + j] = rows[:, j, :]
 
-        def load_w(g):
-            rows = keep.tile([P, PACK, M], F32, name=f"w_{g}")
-            nc.sync.dma_start(out=rows[:], in_=w_rows[g])
-            w_sb.append(rows)
+        def load_w(g, m0, m1):
+            rows = keep.tile([P, PACK, m1 - m0], F32, name=f"w_{g}_{m0}")
+            nc.sync.dma_start(out=rows[:], in_=w_rows[g, :, :, m0:m1])
+            return rows
 
         load_x(0, 0, 2)
+        offs_sb = lists.tile([P, G // 16], U16, name="offs_sb")
+        nc.sync.dma_start(offs_sb[:], offs)
         load_x(0, 2, 2)
-        for j in range(PACK):
-            load_x(1, j, 1)
-        load_w(0)
-        load_w(1)
+        w_sb = {(0, 0): load_w(0, 0, P)}
+        load_x(1, 0, 1)
+        load_x(1, 1, 1)
+        w_sb[1, 0] = load_w(1, 0, P)
+        load_x(1, 2, 1)
+        load_x(1, 3, 1)
+        for g in range(PASSES):
+            w_sb[g, 1] = load_w(g, P, M)
         slots_sb = lists.tile([P, G // 16], U16, name="slots_sb")
         nc.sync.dma_start(slots_sb[:], slots)
-        bias_sb = keep.tile([P, BLOCKS], F32, name="bias_sb")
-        nc.sync.dma_start(out=bias_sb[:], in_=bias.rearrange("(p t) o -> p (t o)", t=BLOCKS))
         cache_sb = []
         for t in range(BLOCKS):
             rows = keep.tile([P, T2], F32, name=f"cache_{t}")
             nc.sync.dma_start(out=rows[:], in_=cache_rows[t])
             cache_sb.append(rows)
+
+        identity = keep.tile([P, P], F32, name="identity")
+        make_identity(nc, identity[:])
+        bias_rows = keep.tile([P, P], F32, name="bias_rows")
+        nc.gpsimd.memset(bias_rows[:], 0.0)
+        nc.scalar.dma_start(out=bias_rows[0:BLOCKS, :], in_=bias.rearrange("(t p) o -> t (p o)", p=P))
+        bias_turned = psum.tile([P, P], F32, name="bias_turned")
+        nc.tensor.transpose(bias_turned[:], bias_rows[:], identity[:])
+        bias_sb = keep.tile([P, BLOCKS], F32, name="bias_sb")
+        nc.scalar.copy(bias_sb[:], bias_turned[:, 0:BLOCKS])
 
         def quantize(name, grouped, width):
             codes = keep.tile([P, width], U32, name=f"{name}_codes", align_bytes=64)
@@ -74,59 +86,48 @@ def tile_attend_fill_bias_kernel(tc, xT, w, cache, bias, offs, slots, out):
             )
             return codes, scales
 
-        x_mx, w_mx = [], {}
-
         def gather(g):
             x_grouped = keep.tile([P, G, PACK], BF16, name=f"x_grouped_{g}", align_bytes=64)
             for j in range(PACK):
                 nc.vector.tensor_copy(out=x_grouped[:, :, j], in_=x_sb[g, j].indirect(offs_sb[:]))
             return x_grouped
 
-        def interleave(g, t, parts):
-            w_grouped = keep.tile([P, P, PACK], BF16, name=f"w_grouped_{g}_{t}", align_bytes=64)
-            source = w_sb[g][:].rearrange("p j (m t) -> p t m j", t=BLOCKS)[:, t]
-            for engine, m0, m1 in parts:
-                target = w_grouped[:, m0:m1, :].rearrange("p (c i) j -> p c j i", i=4)
-                rows = source[:, m0:m1, :].rearrange("p (c i) j -> p c j i", i=4)
-                if engine == "scalar":
-                    nc.scalar.activation(target, rows, COPY)
-                else:
-                    nc.vector.tensor_copy(out=target, in_=rows)
+        def interleave(name, rows, width, engine):
+            w_grouped = keep.tile([P, width, PACK], BF16, name=f"{name}_grouped", align_bytes=64)
+            target = w_grouped[:].rearrange("p (c i) j -> p c j i", i=4)
+            source = rows[:].rearrange("p j (c i) -> p c j i", i=4)
+            if engine == "scalar":
+                nc.scalar.activation(target, source, COPY)
+            else:
+                nc.vector.tensor_copy(out=target, in_=source)
             return w_grouped
 
         pieces = [(0, 0, G // 2), (0, G // 2, G), (1, 0, G)]
         acc = [psum.tile([P, n1 - n0], F32, name=f"acc_{t}_{n0}") for t, n0, n1 in pieces]
 
-        def multiply(g, t):
-            w_codes, w_scales = w_mx[g, t]
-            x_codes, x_scales = x_mx[g]
+        def multiply(g, t, w_codes, w_scales, x_mx):
+            x_codes, x_scales = x_mx
             for i, (block, n0, n1) in enumerate(pieces):
                 if block == t:
                     nc.tensor.matmul_mx(
                         out=acc[i][:],
-                        lhsT=w_codes[:].bitcast(FP8X4),
-                        lhsT_scale=w_scales[:],
+                        lhsT=w_codes.bitcast(FP8X4),
+                        lhsT_scale=w_scales,
                         rhs=x_codes[:, n0:n1].bitcast(FP8X4),
                         rhs_scale=x_scales[:, n0:n1],
                         start=(g == 0),
                         stop=(g == PASSES - 1),
                     )
 
-        x0 = gather(0)
-        x_mx.append(quantize("x0", x0, G))
-        x1 = gather(1)
-        x_mx.append(quantize("x1", x1, G))
-        wg = {}
-        for t in range(BLOCKS):
-            wg[0, t] = interleave(0, t, [("vector" if t == 0 else "scalar", 0, P)])
-        for t in range(BLOCKS):
-            w_mx[0, t] = quantize(f"w0{t}", wg[0, t], P)
-            multiply(0, t)
-        wg[1, 0] = interleave(1, 0, [("scalar", 0, P // 2), ("vector", P // 2, P)])
-        wg[1, 1] = interleave(1, 1, [("scalar", 0, P)])
-        for t in range(BLOCKS):
-            w_mx[1, t] = quantize(f"w1{t}", wg[1, t], P)
-            multiply(1, t)
+        x_mx = []
+        for g in range(PASSES):
+            x_mx.append(quantize(f"x{g}", gather(g), G))
+            codes, scales = quantize(f"w{g}0", interleave(f"w{g}0", w_sb[g, 0], P, "scalar"), P)
+            multiply(g, 0, codes[:], scales[:], x_mx[g])
+        for g in range(PASSES):
+            engine = "scalar" if g == 0 else "vector"
+            codes, scales = quantize(f"w{g}1", interleave(f"w{g}1", w_sb[g, 1], P, engine), P)
+            multiply(g, 1, codes[:], scales[:], x_mx[g])
 
         for t in range(BLOCKS):
             y = keep.tile([P, G], F32, name=f"y_{t}")

@@ -50,14 +50,13 @@ def tile_attend_fill_bias_kernel(tc, xT, w, cache, bias, offs, slots, out):
         offs_sb = lists.tile([P, G // 16], U16, name="offs_sb")
         nc.sync.dma_start(offs_sb[:], offs)
         load_x(0, 2, 2)
-        w_sb = {(0, 0): load_w(0, 0, P)}
-        load_x(1, 0, 1)
-        load_x(1, 1, 1)
-        w_sb[1, 0] = load_w(1, 0, P)
+        load_x(1, 0, 2)
         load_x(1, 2, 1)
         load_x(1, 3, 1)
-        for g in range(PASSES):
-            w_sb[g, 1] = load_w(g, P, M)
+        w0_sb = load_w(0, 0, M)
+        w_sb = {(0, t): w0_sb[:, :, t * P : (t + 1) * P] for t in range(BLOCKS)}
+        for t in range(BLOCKS):
+            w_sb[1, t] = load_w(1, t * P, (t + 1) * P)[:]
         slots_sb = lists.tile([P, G // 16], U16, name="slots_sb")
         nc.sync.dma_start(slots_sb[:], slots)
         cache_sb = []
@@ -84,55 +83,74 @@ def tile_attend_fill_bias_kernel(tc, xT, w, cache, bias, offs, slots, out):
                 scales=scales[:],
                 in_=grouped[:].rearrange("p n j -> p (n j)"),
             )
-            return codes, scales
+            return codes[:], scales[:]
 
-        def gather(g):
-            x_grouped = keep.tile([P, G, PACK], BF16, name=f"x_grouped_{g}", align_bytes=64)
-            for j in range(PACK):
-                nc.vector.tensor_copy(out=x_grouped[:, :, j], in_=x_sb[g, j].indirect(offs_sb[:]))
-            return x_grouped
+        def gather(planes, g, j, n0, n1):
+            nc.vector.tensor_copy(
+                out=planes[:, j, :], in_=x_sb[g, j].indirect(offs_sb[:, n0 // 16 : n1 // 16])
+            )
 
         def interleave(name, rows, width, engine):
-            w_grouped = keep.tile([P, width, PACK], BF16, name=f"{name}_grouped", align_bytes=64)
-            target = w_grouped[:].rearrange("p (c i) j -> p c j i", i=4)
-            source = rows[:].rearrange("p j (c i) -> p c j i", i=4)
+            grouped = keep.tile([P, width, PACK], BF16, name=f"{name}_grouped", align_bytes=64)
+            target = grouped[:].rearrange("p (c i) j -> p c j i", i=4)
+            source = rows.rearrange("p j (c i) -> p c j i", i=4)
             if engine == "scalar":
                 nc.scalar.activation(target, source, COPY)
             else:
                 nc.vector.tensor_copy(out=target, in_=source)
-            return w_grouped
+            return grouped
 
-        pieces = [(0, 0, G // 2), (0, G // 2, G), (1, 0, G)]
-        acc = [psum.tile([P, n1 - n0], F32, name=f"acc_{t}_{n0}") for t, n0, n1 in pieces]
+        halves = [(0, G // 2), (G // 2, G)]
+        acc = {
+            (t, h): psum.tile([P, G // 2], F32, name=f"acc_{t}_{h}")
+            for t in range(BLOCKS)
+            for h in range(2)
+        }
 
-        def multiply(g, t, w_codes, w_scales, x_mx):
-            x_codes, x_scales = x_mx
-            for i, (block, n0, n1) in enumerate(pieces):
-                if block == t:
-                    nc.tensor.matmul_mx(
-                        out=acc[i][:],
-                        lhsT=w_codes.bitcast(FP8X4),
-                        lhsT_scale=w_scales,
-                        rhs=x_codes[:, n0:n1].bitcast(FP8X4),
-                        rhs_scale=x_scales[:, n0:n1],
-                        start=(g == 0),
-                        stop=(g == PASSES - 1),
-                    )
+        def multiply(g, t, h, w_mx, x_mx):
+            nc.tensor.matmul_mx(
+                out=acc[t, h][:],
+                lhsT=w_mx[0].bitcast(FP8X4),
+                lhsT_scale=w_mx[1],
+                rhs=x_mx[0].bitcast(FP8X4),
+                rhs_scale=x_mx[1],
+                start=(g == 0),
+                stop=(g == PASSES - 1),
+            )
 
-        x_mx = []
-        for g in range(PASSES):
-            x_mx.append(quantize(f"x{g}", gather(g), G))
-            codes, scales = quantize(f"w{g}0", interleave(f"w{g}0", w_sb[g, 0], P, "scalar"), P)
-            multiply(g, 0, codes[:], scales[:], x_mx[g])
-        for g in range(PASSES):
-            engine = "scalar" if g == 0 else "vector"
-            codes, scales = quantize(f"w{g}1", interleave(f"w{g}1", w_sb[g, 1], P, engine), P)
-            multiply(g, 1, codes[:], scales[:], x_mx[g])
+        x_mx = {}
+        planes = keep.tile([P, PACK, G], F32, name="planes_0")
+        for j in range(PACK):
+            gather(planes, 0, j, 0, G)
+        codes, scales = quantize("x0", interleave("x0", planes[:], G, "scalar"), G)
+        for h, (n0, n1) in enumerate(halves):
+            x_mx[0, h] = codes[:, n0:n1], scales[:, n0:n1]
+
+        planes = keep.tile([P, 2, G], F32, name="planes_1")
+        grouped = keep.tile([P, G, PACK], BF16, name="x1_grouped", align_bytes=64)
+        for j in range(2):
+            gather(planes, 1, j, 0, G)
+        nc.scalar.activation(
+            grouped[:, :, 0:2].rearrange("p (c i) j -> p c j i", i=4),
+            planes[:].rearrange("p j (c i) -> p c j i", i=4),
+            COPY,
+        )
+        for j in range(2, PACK):
+            nc.vector.tensor_copy(out=grouped[:, :, j], in_=x_sb[1, j].indirect(offs_sb[:]))
+        codes, scales = quantize("x1", grouped, G)
+        for h, (n0, n1) in enumerate(halves):
+            x_mx[1, h] = codes[:, n0:n1], scales[:, n0:n1]
+
+        for t in range(BLOCKS):
+            w_grouped = [interleave(f"w0{t}", w_sb[0, t], P, "scalar"), interleave("w1", w_sb[1, t], P, "vector")]
+            for g in range(PASSES):
+                w_mx = quantize(f"w{g}{t}", w_grouped[g], P)
+                for h in range(2):
+                    multiply(g, t, h, w_mx, x_mx[g, h])
 
         for t in range(BLOCKS):
             y = keep.tile([P, G], F32, name=f"y_{t}")
-            for i, (block, n0, n1) in enumerate(pieces):
-                if block == t:
-                    nc.scalar.activation(y[:, n0:n1], acc[i][:], IDENTITY, bias=bias_sb[:, t : t + 1])
+            for h, (n0, n1) in enumerate(halves):
+                nc.scalar.activation(y[:, n0:n1], acc[t, h][:], IDENTITY, bias=bias_sb[:, t : t + 1])
             nc.vector.tensor_copy(out=cache_sb[t][:].indirect(slots_sb[:]), in_=y[:])
             nc.sync.dma_start(out=out_rows[t], in_=cache_sb[t][:])

@@ -53,10 +53,10 @@ def tile_attend_fill_bias_kernel(tc, xT, w, cache, bias, offs, slots, out):
         load_x(1, 0, 2)
         load_x(1, 2, 1)
         load_x(1, 3, 1)
-        w0_sb = load_w(0, 0, M)
-        w_sb = {(0, t): w0_sb[:, :, t * P : (t + 1) * P] for t in range(BLOCKS)}
+        w_sb = {}
         for t in range(BLOCKS):
-            w_sb[1, t] = load_w(1, t * P, (t + 1) * P)[:]
+            for g in range(PASSES):
+                w_sb[g, t] = load_w(g, t * P, (t + 1) * P)[:]
         slots_sb = lists.tile([P, G // 16], U16, name="slots_sb")
         nc.sync.dma_start(slots_sb[:], slots)
         cache_sb = []
@@ -81,7 +81,7 @@ def tile_attend_fill_bias_kernel(tc, xT, w, cache, bias, offs, slots, out):
             nc.vector.quantize_mx(
                 out=codes[:].bitcast(FP8X4),
                 scales=scales[:],
-                in_=grouped[:].rearrange("p n j -> p (n j)"),
+                in_=grouped.rearrange("p n j -> p (n j)"),
             )
             return codes[:], scales[:]
 
@@ -90,15 +90,16 @@ def tile_attend_fill_bias_kernel(tc, xT, w, cache, bias, offs, slots, out):
                 out=planes[:, j, :], in_=x_sb[g, j].indirect(offs_sb[:, n0 // 16 : n1 // 16])
             )
 
-        def interleave(name, rows, width, engine):
+        def interleave(name, rows, width, on_vector):
             grouped = keep.tile([P, width, PACK], BF16, name=f"{name}_grouped", align_bytes=64)
             target = grouped[:].rearrange("p (c i) j -> p c j i", i=4)
             source = rows.rearrange("p j (c i) -> p c j i", i=4)
-            if engine == "scalar":
-                nc.scalar.activation(target, source, COPY)
-            else:
-                nc.vector.tensor_copy(out=target, in_=source)
-            return grouped
+            cut = on_vector // 4
+            if cut > 0:
+                nc.vector.tensor_copy(out=target[:, 0:cut], in_=source[:, 0:cut])
+            if on_vector < width:
+                nc.scalar.activation(target[:, cut:], source[:, cut:], COPY)
+            return grouped[:]
 
         halves = [(0, G // 2), (G // 2, G)]
         acc = {
@@ -122,7 +123,7 @@ def tile_attend_fill_bias_kernel(tc, xT, w, cache, bias, offs, slots, out):
         planes = keep.tile([P, PACK, G], F32, name="planes_0")
         for j in range(PACK):
             gather(planes, 0, j, 0, G)
-        codes, scales = quantize("x0", interleave("x0", planes[:], G, "scalar"), G)
+        codes, scales = quantize("x0", interleave("x0", planes[:], G, 0), G)
         for h, (n0, n1) in enumerate(halves):
             x_mx[0, h] = codes[:, n0:n1], scales[:, n0:n1]
 
@@ -135,14 +136,16 @@ def tile_attend_fill_bias_kernel(tc, xT, w, cache, bias, offs, slots, out):
             planes[:].rearrange("p j (c i) -> p c j i", i=4),
             COPY,
         )
-        for j in range(2, PACK):
-            nc.vector.tensor_copy(out=grouped[:, :, j], in_=x_sb[1, j].indirect(offs_sb[:]))
-        codes, scales = quantize("x1", grouped, G)
+        nc.vector.tensor_copy(out=grouped[:, :, 2], in_=x_sb[1, 2].indirect(offs_sb[:]))
+        for n0, n1 in halves:
+            nc.vector.tensor_copy(
+                out=grouped[:, n0:n1, 3], in_=x_sb[1, 3].indirect(offs_sb[:, n0 // 16 : n1 // 16])
+            )
         for h, (n0, n1) in enumerate(halves):
-            x_mx[1, h] = codes[:, n0:n1], scales[:, n0:n1]
+            x_mx[1, h] = quantize(f"x1{h}", grouped[:, n0:n1, :], G // 2)
 
         for t in range(BLOCKS):
-            w_grouped = [interleave(f"w0{t}", w_sb[0, t], P, "scalar"), interleave("w1", w_sb[1, t], P, "vector")]
+            w_grouped = [interleave(f"w0{t}", w_sb[0, t], P, 0), interleave(f"w1{t}", w_sb[1, t], P, P)]
             for g in range(PASSES):
                 w_mx = quantize(f"w{g}{t}", w_grouped[g], P)
                 for h in range(2):

@@ -17,6 +17,7 @@ PACK = 4
 G, T, T2, D, M = 256, 1024, 1024, 1024, 256
 PASSES = D // (P * PACK)
 BLOCKS = M // P
+W_HEAD = PACK * M - P
 
 FLOPS = 2 * D * M * G
 
@@ -24,7 +25,7 @@ FLOPS = 2 * D * M * G
 def tile_attend_fill_bias_kernel(tc, xT, w, cache, bias, offs, slots, out):
     nc = tc.nc
     x_rows = xT.rearrange("(g p j) n -> g p j n", p=P, j=PACK)
-    w_rows = w.rearrange("(g p j) m -> g p j m", p=P, j=PACK)
+    w_runs = w.rearrange("(g p j) m -> p g (j m)", p=P, j=PACK)
     cache_rows = cache.rearrange("(t p) n -> t p n", p=P)
     out_rows = out.rearrange("(t p) n -> t p n", p=P)
 
@@ -41,11 +42,6 @@ def tile_attend_fill_bias_kernel(tc, xT, w, cache, bias, offs, slots, out):
             for j in range(count):
                 x_sb[g, j0 + j] = rows[:, j, :]
 
-        def load_w(g, m0, m1):
-            rows = keep.tile([P, PACK, m1 - m0], F32, name=f"w_{g}_{m0}")
-            nc.sync.dma_start(out=rows[:], in_=w_rows[g, :, :, m0:m1])
-            return rows
-
         load_x(0, 0, 2)
         offs_sb = lists.tile([P, G // 16], U16, name="offs_sb")
         nc.sync.dma_start(offs_sb[:], offs)
@@ -53,10 +49,15 @@ def tile_attend_fill_bias_kernel(tc, xT, w, cache, bias, offs, slots, out):
         load_x(1, 0, 2)
         load_x(1, 2, 1)
         load_x(1, 3, 1)
-        w_sb = {}
-        for t in range(BLOCKS):
-            for g in range(PASSES):
-                w_sb[g, t] = load_w(g, t * P, (t + 1) * P)[:]
+        w_all = keep.tile([P, PASSES, PACK * M], F32, name="w_all")
+        for g in range(PASSES):
+            nc.sync.dma_start(out=w_all[:, g, 0:W_HEAD], in_=w_runs[:, g, 0:W_HEAD])
+        nc.sync.dma_start(out=w_all[:, :, W_HEAD:], in_=w_runs[:, :, W_HEAD:])
+        w_sb = {
+            (g, t): w_all[:, g, :].rearrange("p (j m) -> p j m", j=PACK)[:, :, t * P : (t + 1) * P]
+            for g in range(PASSES)
+            for t in range(BLOCKS)
+        }
         slots_sb = lists.tile([P, G // 16], U16, name="slots_sb")
         nc.sync.dma_start(slots_sb[:], slots)
         cache_sb = []
@@ -144,12 +145,26 @@ def tile_attend_fill_bias_kernel(tc, xT, w, cache, bias, offs, slots, out):
         for h, (n0, n1) in enumerate(halves):
             x_mx[1, h] = quantize(f"x1{h}", grouped[:, n0:n1, :], G // 2)
 
-        for t in range(BLOCKS):
-            w_grouped = [interleave(f"w0{t}", w_sb[0, t], P, 0), interleave(f"w1{t}", w_sb[1, t], P, P)]
-            for g in range(PASSES):
-                w_mx = quantize(f"w{g}{t}", w_grouped[g], P)
-                for h in range(2):
-                    multiply(g, t, h, w_mx, x_mx[g, h])
+        def finish(g, t, grouped):
+            w_mx = quantize(f"w{g}{t}", grouped, P)
+            for h in range(2):
+                multiply(g, t, h, w_mx, x_mx[g, h])
+
+        def interleave_pair(grouped, rows, j0):
+            nc.scalar.activation(
+                grouped[:, :, j0 : j0 + 2].rearrange("p (c i) j -> p c j i", i=4),
+                rows[:, j0 : j0 + 2, :].rearrange("p j (c i) -> p c j i", i=4),
+                COPY,
+            )
+
+        w01_grouped = keep.tile([P, P, PACK], BF16, name="w01_grouped", align_bytes=64)
+        finish(0, 0, interleave("w00", w_sb[0, 0], P, P))
+        interleave_pair(w01_grouped, w_sb[0, 1], 0)
+        finish(1, 0, interleave("w10", w_sb[1, 0], P, 96))
+        interleave_pair(w01_grouped, w_sb[0, 1], 2)
+        w11_grouped = interleave("w11", w_sb[1, 1], P, P)
+        finish(0, 1, w01_grouped[:])
+        finish(1, 1, w11_grouped)
 
         for t in range(BLOCKS):
             y = keep.tile([P, G], F32, name=f"y_{t}")

@@ -17,7 +17,6 @@ PACK = 4
 G, T, T2, D, M = 256, 1024, 1024, 1024, 256
 PASSES = D // (P * PACK)
 BLOCKS = M // P
-W_HEAD = PACK * M - P
 
 FLOPS = 2 * D * M * G
 
@@ -25,7 +24,7 @@ FLOPS = 2 * D * M * G
 def tile_attend_fill_bias_kernel(tc, xT, w, cache, bias, offs, slots, out):
     nc = tc.nc
     x_rows = xT.rearrange("(g p j) n -> g p j n", p=P, j=PACK)
-    w_runs = w.rearrange("(g p j) m -> p g (j m)", p=P, j=PACK)
+    w_rows = w.rearrange("(g p j) m -> g p j m", p=P, j=PACK)
     cache_rows = cache.rearrange("(t p) n -> t p n", p=P)
     out_rows = out.rearrange("(t p) n -> t p n", p=P)
 
@@ -42,6 +41,11 @@ def tile_attend_fill_bias_kernel(tc, xT, w, cache, bias, offs, slots, out):
             for j in range(count):
                 x_sb[g, j0 + j] = rows[:, j, :]
 
+        def load_w(g, m0, m1):
+            rows = keep.tile([P, PACK, m1 - m0], F32, name=f"w_{g}_{m0}", align_bytes=64)
+            nc.sync.dma_start(out=rows[:], in_=w_rows[g, :, :, m0:m1])
+            return rows
+
         load_x(0, 0, 2)
         offs_sb = lists.tile([P, G // 16], U16, name="offs_sb")
         nc.sync.dma_start(offs_sb[:], offs)
@@ -49,15 +53,10 @@ def tile_attend_fill_bias_kernel(tc, xT, w, cache, bias, offs, slots, out):
         load_x(1, 0, 2)
         load_x(1, 2, 1)
         load_x(1, 3, 1)
-        w_all = keep.tile([P, PASSES, PACK * M], F32, name="w_all")
-        for g in range(PASSES):
-            nc.sync.dma_start(out=w_all[:, g, 0:W_HEAD], in_=w_runs[:, g, 0:W_HEAD])
-        nc.sync.dma_start(out=w_all[:, :, W_HEAD:], in_=w_runs[:, :, W_HEAD:])
-        w_sb = {
-            (g, t): w_all[:, g, :].rearrange("p (j m) -> p j m", j=PACK)[:, :, t * P : (t + 1) * P]
-            for g in range(PASSES)
-            for t in range(BLOCKS)
-        }
+        w0_sb = load_w(0, 0, M)
+        w_sb = {(0, t): w0_sb[:, :, t * P : (t + 1) * P] for t in range(BLOCKS)}
+        for t in range(BLOCKS):
+            w_sb[1, t] = load_w(1, t * P, (t + 1) * P)[:]
         slots_sb = lists.tile([P, G // 16], U16, name="slots_sb")
         nc.sync.dma_start(slots_sb[:], slots)
         cache_sb = []
@@ -69,7 +68,7 @@ def tile_attend_fill_bias_kernel(tc, xT, w, cache, bias, offs, slots, out):
         identity = keep.tile([P, P], F32, name="identity")
         make_identity(nc, identity[:])
         bias_rows = keep.tile([P, P], F32, name="bias_rows")
-        nc.gpsimd.memset(bias_rows[:], 0.0)
+        nc.vector.memset(bias_rows[:], 0.0)
         nc.scalar.dma_start(out=bias_rows[0:BLOCKS, :], in_=bias.rearrange("(t p) o -> t (p o)", p=P))
         bias_turned = psum.tile([P, P], F32, name="bias_turned")
         nc.tensor.transpose(bias_turned[:], bias_rows[:], identity[:])
@@ -86,13 +85,8 @@ def tile_attend_fill_bias_kernel(tc, xT, w, cache, bias, offs, slots, out):
             )
             return codes[:], scales[:]
 
-        def gather(planes, g, j, n0, n1):
-            nc.vector.tensor_copy(
-                out=planes[:, j, :], in_=x_sb[g, j].indirect(offs_sb[:, n0 // 16 : n1 // 16])
-            )
-
         def interleave(name, rows, width, on_vector):
-            grouped = keep.tile([P, width, PACK], BF16, name=f"{name}_grouped", align_bytes=64)
+            grouped = keep.tile([P, width, PACK], BF16, name=name, align_bytes=64)
             target = grouped[:].rearrange("p (c i) j -> p c j i", i=4)
             source = rows.rearrange("p j (c i) -> p c j i", i=4)
             cut = on_vector // 4
@@ -120,36 +114,6 @@ def tile_attend_fill_bias_kernel(tc, xT, w, cache, bias, offs, slots, out):
                 stop=(g == PASSES - 1),
             )
 
-        x_mx = {}
-        planes = keep.tile([P, PACK, G], F32, name="planes_0")
-        for j in range(PACK):
-            gather(planes, 0, j, 0, G)
-        codes, scales = quantize("x0", interleave("x0", planes[:], G, 0), G)
-        for h, (n0, n1) in enumerate(halves):
-            x_mx[0, h] = codes[:, n0:n1], scales[:, n0:n1]
-
-        planes = keep.tile([P, 2, G], F32, name="planes_1")
-        grouped = keep.tile([P, G, PACK], BF16, name="x1_grouped", align_bytes=64)
-        for j in range(2):
-            gather(planes, 1, j, 0, G)
-        nc.scalar.activation(
-            grouped[:, :, 0:2].rearrange("p (c i) j -> p c j i", i=4),
-            planes[:].rearrange("p j (c i) -> p c j i", i=4),
-            COPY,
-        )
-        nc.vector.tensor_copy(out=grouped[:, :, 2], in_=x_sb[1, 2].indirect(offs_sb[:]))
-        for n0, n1 in halves:
-            nc.vector.tensor_copy(
-                out=grouped[:, n0:n1, 3], in_=x_sb[1, 3].indirect(offs_sb[:, n0 // 16 : n1 // 16])
-            )
-        for h, (n0, n1) in enumerate(halves):
-            x_mx[1, h] = quantize(f"x1{h}", grouped[:, n0:n1, :], G // 2)
-
-        def finish(g, t, grouped):
-            w_mx = quantize(f"w{g}{t}", grouped, P)
-            for h in range(2):
-                multiply(g, t, h, w_mx, x_mx[g, h])
-
         def interleave_pair(grouped, rows, j0):
             nc.scalar.activation(
                 grouped[:, :, j0 : j0 + 2].rearrange("p (c i) j -> p c j i", i=4),
@@ -157,14 +121,32 @@ def tile_attend_fill_bias_kernel(tc, xT, w, cache, bias, offs, slots, out):
                 COPY,
             )
 
-        w01_grouped = keep.tile([P, P, PACK], BF16, name="w01_grouped", align_bytes=64)
-        finish(0, 0, interleave("w00", w_sb[0, 0], P, P))
-        interleave_pair(w01_grouped, w_sb[0, 1], 0)
-        finish(1, 0, interleave("w10", w_sb[1, 0], P, 96))
-        interleave_pair(w01_grouped, w_sb[0, 1], 2)
-        w11_grouped = interleave("w11", w_sb[1, 1], P, P)
-        finish(0, 1, w01_grouped[:])
-        finish(1, 1, w11_grouped)
+        x_mx = {}
+        for g in range(PASSES):
+            planes = keep.tile([P, 2, G], F32, name=f"planes_{g}")
+            grouped = keep.tile([P, G, PACK], BF16, name=f"x{g}_grouped", align_bytes=64)
+            for j in range(2):
+                nc.vector.tensor_copy(out=planes[:, j, :], in_=x_sb[g, j].indirect(offs_sb[:]))
+            interleave_pair(grouped, planes[:], 0)
+            nc.vector.tensor_copy(out=grouped[:, :, 2], in_=x_sb[g, 2].indirect(offs_sb[:]))
+            for n0, n1 in halves:
+                nc.vector.tensor_copy(
+                    out=grouped[:, n0:n1, 3], in_=x_sb[g, 3].indirect(offs_sb[:, n0 // 16 : n1 // 16])
+                )
+            for h, (n0, n1) in enumerate(halves):
+                x_mx[g, h] = quantize(f"x{g}{h}", grouped[:, n0:n1, :], G // 2)
+
+        def finish(g, t, grouped):
+            w_mx = quantize(f"w{g}{t}", grouped, P)
+            for h in range(2):
+                multiply(g, t, h, w_mx, x_mx[g, h])
+
+        w_grouped = [interleave("w00_grouped", w_sb[0, 0], P, 0), interleave("w1_grouped", w_sb[1, 0], P, 96)]
+        for g in range(PASSES):
+            finish(g, 0, w_grouped[g])
+        w_grouped = [interleave("w_1_0", w_sb[0, 1], P, 0), interleave("w1_grouped", w_sb[1, 1], P, 64)]
+        for g in range(PASSES):
+            finish(g, 1, w_grouped[g])
 
         for t in range(BLOCKS):
             y = keep.tile([P, G], F32, name=f"y_{t}")

@@ -17,6 +17,8 @@ PACK = 4
 G, T, T2, D, M = 256, 1024, 1024, 1024, 256
 PASSES = D // (P * PACK)
 BLOCKS = M // P
+HALF = G // 2
+SHARE = 88
 
 FLOPS = 2 * D * M * G
 
@@ -32,6 +34,9 @@ def tile_attend_fill_bias_kernel(tc, xT, w, cache, bias, offs, slots, out):
         lists = ctx.enter_context(tc.tile_pool(name="lists", bufs=1))
         keep = ctx.enter_context(tc.tile_pool(name="keep", bufs=1))
         psum = ctx.enter_context(tc.psum_pool(name="psum", bufs=1))
+
+        bias_rows = keep.tile([P, P], F32, name="bias_rows")
+        nc.gpsimd.memset(bias_rows[:], 0.0)
 
         x_sb = {}
 
@@ -49,6 +54,7 @@ def tile_attend_fill_bias_kernel(tc, xT, w, cache, bias, offs, slots, out):
         load_x(0, 0, 2)
         offs_sb = lists.tile([P, G // 16], U16, name="offs_sb")
         nc.sync.dma_start(offs_sb[:], offs)
+        nc.sync.dma_start(out=bias_rows[0:BLOCKS, :], in_=bias.rearrange("(t p) o -> t (p o)", p=P))
         load_x(0, 2, 2)
         load_x(1, 0, 2)
         load_x(1, 2, 1)
@@ -57,19 +63,14 @@ def tile_attend_fill_bias_kernel(tc, xT, w, cache, bias, offs, slots, out):
         w_sb = {(0, t): w0_sb[:, :, t * P : (t + 1) * P] for t in range(BLOCKS)}
         for t in range(BLOCKS):
             w_sb[1, t] = load_w(1, t * P, (t + 1) * P)[:]
+        cache_sb = [keep.tile([P, T2], F32, name=f"cache_{t}") for t in range(BLOCKS)]
+        nc.sync.dma_start(out=cache_sb[0][:], in_=cache_rows[0])
         slots_sb = lists.tile([P, G // 16], U16, name="slots_sb")
         nc.sync.dma_start(slots_sb[:], slots)
-        cache_sb = []
-        for t in range(BLOCKS):
-            rows = keep.tile([P, T2], F32, name=f"cache_{t}")
-            nc.sync.dma_start(out=rows[:], in_=cache_rows[t])
-            cache_sb.append(rows)
+        nc.sync.dma_start(out=cache_sb[1][:], in_=cache_rows[1])
 
         identity = keep.tile([P, P], F32, name="identity")
         make_identity(nc, identity[:])
-        bias_rows = keep.tile([P, P], F32, name="bias_rows")
-        nc.vector.memset(bias_rows[:], 0.0)
-        nc.scalar.dma_start(out=bias_rows[0:BLOCKS, :], in_=bias.rearrange("(t p) o -> t (p o)", p=P))
         bias_turned = psum.tile([P, P], F32, name="bias_turned")
         nc.tensor.transpose(bias_turned[:], bias_rows[:], identity[:])
         bias_sb = keep.tile([P, BLOCKS], F32, name="bias_sb")
@@ -85,16 +86,13 @@ def tile_attend_fill_bias_kernel(tc, xT, w, cache, bias, offs, slots, out):
             )
             return codes[:], scales[:]
 
-        def interleave(name, rows, width, on_vector):
-            grouped = keep.tile([P, width, PACK], BF16, name=name, align_bytes=64)
-            target = grouped[:].rearrange("p (c i) j -> p c j i", i=4)
+        def weave(engine, grouped, rows):
+            target = grouped.rearrange("p (c i) j -> p c j i", i=4)
             source = rows.rearrange("p j (c i) -> p c j i", i=4)
-            cut = on_vector // 4
-            if cut > 0:
-                nc.vector.tensor_copy(out=target[:, 0:cut], in_=source[:, 0:cut])
-            if on_vector < width:
-                nc.scalar.activation(target[:, cut:], source[:, cut:], COPY)
-            return grouped[:]
+            if engine is nc.vector:
+                nc.vector.tensor_copy(out=target, in_=source)
+            else:
+                nc.scalar.activation(target, source, COPY)
 
         halves = [(0, G // 2), (G // 2, G)]
         acc = {
@@ -114,39 +112,48 @@ def tile_attend_fill_bias_kernel(tc, xT, w, cache, bias, offs, slots, out):
                 stop=(g == PASSES - 1),
             )
 
-        def interleave_pair(grouped, rows, j0):
-            nc.scalar.activation(
-                grouped[:, :, j0 : j0 + 2].rearrange("p (c i) j -> p c j i", i=4),
-                rows[:, j0 : j0 + 2, :].rearrange("p j (c i) -> p c j i", i=4),
-                COPY,
+        x_grouped = keep.tile([P, 2, PASSES, HALF, PACK], BF16, name="x_grouped", align_bytes=64)
+
+        def gather_pair(g, j0):
+            planes = keep.tile([P, 2, G], F32, name=f"planes_{g}_{j0}")
+            for j in range(2):
+                nc.vector.tensor_copy(out=planes[:, j, :], in_=x_sb[g, j0 + j].indirect(offs_sb[:]))
+            nc.scalar.copy(
+                x_grouped[:, :, g, :, j0 : j0 + 2].rearrange("p h (c i) j -> p h c j i", i=4),
+                planes[:].rearrange("p j (h c i) -> p h c j i", h=2, i=4),
             )
 
+        gather_pair(0, 0)
+        gather_pair(0, 2)
+        gather_pair(1, 0)
+        nc.vector.tensor_copy(out=x_grouped[:, :, 1, :, 2], in_=x_sb[1, 2].indirect(offs_sb[:]))
+        for h, (n0, n1) in enumerate(halves):
+            nc.vector.tensor_copy(
+                out=x_grouped[:, h, 1, :, 3], in_=x_sb[1, 3].indirect(offs_sb[:, n0 // 16 : n1 // 16])
+            )
         x_mx = {}
-        for g in range(PASSES):
-            planes = keep.tile([P, 2, G], F32, name=f"planes_{g}")
-            grouped = keep.tile([P, G, PACK], BF16, name=f"x{g}_grouped", align_bytes=64)
-            for j in range(2):
-                nc.vector.tensor_copy(out=planes[:, j, :], in_=x_sb[g, j].indirect(offs_sb[:]))
-            interleave_pair(grouped, planes[:], 0)
-            nc.vector.tensor_copy(out=grouped[:, :, 2], in_=x_sb[g, 2].indirect(offs_sb[:]))
-            for n0, n1 in halves:
-                nc.vector.tensor_copy(
-                    out=grouped[:, n0:n1, 3], in_=x_sb[g, 3].indirect(offs_sb[:, n0 // 16 : n1 // 16])
-                )
-            for h, (n0, n1) in enumerate(halves):
-                x_mx[g, h] = quantize(f"x{g}{h}", grouped[:, n0:n1, :], G // 2)
+        for h in range(2):
+            codes, scales = quantize(f"x{h}", x_grouped[:, h].rearrange("p g n j -> p (g n) j"), PASSES * HALF)
+            for g in range(PASSES):
+                x_mx[g, h] = (codes[:, g * HALF : (g + 1) * HALF], scales[:, g * HALF : (g + 1) * HALF])
 
-        def finish(g, t, grouped):
-            w_mx = quantize(f"w{g}{t}", grouped, P)
+        first = [keep.tile([P, P, PACK], BF16, name=f"w{g}0_grouped", align_bytes=64) for g in range(PASSES)]
+        weave(nc.scalar, first[0][:], w_sb[0, 0])
+        weave(nc.vector, first[1][:, 0:SHARE], w_sb[1, 0][:, :, 0:SHARE])
+        weave(nc.scalar, first[1][:, SHARE:P], w_sb[1, 0][:, :, SHARE:P])
+        for g in range(PASSES):
+            w_mx = quantize(f"w{g}0", first[g][:], P)
             for h in range(2):
-                multiply(g, t, h, w_mx, x_mx[g, h])
+                multiply(g, 0, h, w_mx, x_mx[g, h])
 
-        w_grouped = [interleave("w00_grouped", w_sb[0, 0], P, 0), interleave("w1_grouped", w_sb[1, 0], P, 96)]
-        for g in range(PASSES):
-            finish(g, 0, w_grouped[g])
-        w_grouped = [interleave("w_1_0", w_sb[0, 1], P, 0), interleave("w1_grouped", w_sb[1, 1], P, 64)]
-        for g in range(PASSES):
-            finish(g, 1, w_grouped[g])
+        second = keep.tile([P, PASSES, P, PACK], BF16, name="w_1_0", align_bytes=64)
+        weave(nc.scalar, second[:, 0], w_sb[0, 1])
+        weave(nc.vector, second[:, 1], w_sb[1, 1])
+        codes, scales = quantize("w1", second[:].rearrange("p g m j -> p (g m) j"), PASSES * P)
+        for h in range(2):
+            for g in range(PASSES):
+                w_mx = (codes[:, g * P : (g + 1) * P], scales[:, g * P : (g + 1) * P])
+                multiply(g, 1, h, w_mx, x_mx[g, h])
 
         for t in range(BLOCKS):
             y = keep.tile([P, G], F32, name=f"y_{t}")

@@ -1,7 +1,6 @@
 from contextlib import ExitStack
 
 import concourse.mybir as mybir
-from concourse.masks import make_identity
 
 F32 = mybir.dt.float32
 BF16 = mybir.dt.bfloat16
@@ -18,6 +17,7 @@ G, T, T2, D, M = 256, 1024, 1024, 1024, 256
 PASSES = D // (P * PACK)
 BLOCKS = M // P
 HALF = G // 2
+QUAD = 32
 SHARE = 88
 
 FLOPS = 2 * D * M * G
@@ -35,8 +35,8 @@ def tile_attend_fill_bias_kernel(tc, xT, w, cache, bias, offs, slots, out):
         keep = ctx.enter_context(tc.tile_pool(name="keep", bufs=1))
         psum = ctx.enter_context(tc.psum_pool(name="psum", bufs=1))
 
-        bias_rows = keep.tile([P, P], F32, name="bias_rows")
-        nc.gpsimd.memset(bias_rows[:], 0.0)
+        bias_rows = keep.tile([P, BLOCKS, QUAD], F32, name="bias_rows", align_bytes=64)
+        nc.vector.memset(bias_rows[:], 0.0)
 
         x_sb = {}
 
@@ -54,7 +54,7 @@ def tile_attend_fill_bias_kernel(tc, xT, w, cache, bias, offs, slots, out):
         load_x(0, 0, 2)
         offs_sb = lists.tile([P, G // 16], U16, name="offs_sb")
         nc.sync.dma_start(offs_sb[:], offs)
-        nc.sync.dma_start(out=bias_rows[0:BLOCKS, :], in_=bias.rearrange("(t p) o -> t (p o)", p=P))
+        nc.sync.dma_start(out=bias_rows[0:P:QUAD], in_=bias.rearrange("(t q i) o -> q t (i o)", t=BLOCKS, i=QUAD))
         load_x(0, 2, 2)
         load_x(1, 0, 2)
         load_x(1, 2, 1)
@@ -69,12 +69,9 @@ def tile_attend_fill_bias_kernel(tc, xT, w, cache, bias, offs, slots, out):
         nc.sync.dma_start(slots_sb[:], slots)
         nc.sync.dma_start(out=cache_sb[1][:], in_=cache_rows[1])
 
-        identity = keep.tile([P, P], F32, name="identity")
-        make_identity(nc, identity[:])
-        bias_turned = psum.tile([P, P], F32, name="bias_turned")
-        nc.tensor.transpose(bias_turned[:], bias_rows[:], identity[:])
-        bias_sb = keep.tile([P, BLOCKS], F32, name="bias_sb")
-        nc.scalar.copy(bias_sb[:], bias_turned[:, 0:BLOCKS])
+        bias_turned = keep.tile([P, BLOCKS, QUAD], F32, name="bias_turned", align_bytes=64)
+        for t in range(BLOCKS):
+            nc.vector.transpose(bias_turned[:, t, :], bias_rows[:, t, :])
 
         def quantize(name, grouped, width):
             codes = keep.tile([P, width], U32, name=f"{name}_codes", align_bytes=64)
@@ -158,6 +155,6 @@ def tile_attend_fill_bias_kernel(tc, xT, w, cache, bias, offs, slots, out):
         for t in range(BLOCKS):
             y = keep.tile([P, G], F32, name=f"y_{t}")
             for h, (n0, n1) in enumerate(halves):
-                nc.scalar.activation(y[:, n0:n1], acc[t, h][:], IDENTITY, bias=bias_sb[:, t : t + 1])
+                nc.scalar.activation(y[:, n0:n1], acc[t, h][:], IDENTITY, bias=bias_turned[:, t, 0:1])
             nc.vector.tensor_copy(out=cache_sb[t][:].indirect(slots_sb[:]), in_=y[:])
             nc.sync.dma_start(out=out_rows[t], in_=cache_sb[t][:])

@@ -156,5 +156,8 @@ def tile_attend_fill_bias_kernel(tc, xT, w, cache, bias, offs, slots, out):
             y = keep.tile([P, G], F32, name=f"y_{t}")
             for h, (n0, n1) in enumerate(halves):
                 nc.scalar.activation(y[:, n0:n1], acc[t, h][:], IDENTITY, bias=bias_turned[:, t, 0:1])
-            nc.vector.tensor_copy(out=cache_sb[t][:].indirect(slots_sb[:]), in_=y[:])
+            if t == 0:
+                nc.vector.tensor_copy(out=cache_sb[t][:].indirect(slots_sb[:]), in_=y[:])
+            else:
+                nc.scalar.activation(cache_sb[t][:].indirect(slots_sb[:]), y[:], COPY)
             nc.sync.dma_start(out=out_rows[t], in_=cache_sb[t][:])

@@ -19,6 +19,7 @@ BLOCKS = M // P
 HALF = G // 2
 QUAD = 32
 SHARE = 88
+APART = 128 * 1024
 
 FLOPS = 2 * D * M * G
 
@@ -33,6 +34,7 @@ def tile_attend_fill_bias_kernel(tc, xT, w, cache, bias, offs, slots, out):
     with ExitStack() as ctx:
         lists = ctx.enter_context(tc.tile_pool(name="lists", bufs=1))
         keep = ctx.enter_context(tc.tile_pool(name="keep", bufs=1))
+        ends = ctx.enter_context(tc.tile_pool(name="ends", bufs=1))
         psum = ctx.enter_context(tc.psum_pool(name="psum", bufs=1))
 
         bias_rows = keep.tile([P, BLOCKS, QUAD], F32, name="bias_rows", align_bytes=64)
@@ -63,7 +65,7 @@ def tile_attend_fill_bias_kernel(tc, xT, w, cache, bias, offs, slots, out):
         w_sb = {(0, t): w0_sb[:, :, t * P : (t + 1) * P] for t in range(BLOCKS)}
         for t in range(BLOCKS):
             w_sb[1, t] = load_w(1, t * P, (t + 1) * P)[:]
-        cache_sb = [keep.tile([P, T2], F32, name=f"cache_{t}") for t in range(BLOCKS)]
+        cache_sb = [ends.tile([P, T2], F32, name=f"cache_{t}", offset=t * APART) for t in range(BLOCKS)]
         nc.sync.dma_start(out=cache_sb[0][:], in_=cache_rows[0])
         slots_sb = lists.tile([P, G // 16], U16, name="slots_sb")
         nc.sync.dma_start(slots_sb[:], slots)
@@ -146,14 +148,13 @@ def tile_attend_fill_bias_kernel(tc, xT, w, cache, bias, offs, slots, out):
         second = keep.tile([P, PASSES, P, PACK], BF16, name="w_1_0", align_bytes=64)
         weave(nc.scalar, second[:, 0], w_sb[0, 1])
         weave(nc.vector, second[:, 1], w_sb[1, 1])
-        codes, scales = quantize("w1", second[:].rearrange("p g m j -> p (g m) j"), PASSES * P)
-        for h in range(2):
-            for g in range(PASSES):
-                w_mx = (codes[:, g * P : (g + 1) * P], scales[:, g * P : (g + 1) * P])
+        for g in range(PASSES):
+            w_mx = quantize(f"w{g}1", second[:, g], P)
+            for h in range(2):
                 multiply(g, 1, h, w_mx, x_mx[g, h])
 
         for t in range(BLOCKS):
-            y = keep.tile([P, G], F32, name=f"y_{t}")
+            y = ends.tile([P, G], F32, name=f"y_{t}", offset=t * APART + 4 * T2)
             for h, (n0, n1) in enumerate(halves):
                 nc.scalar.activation(y[:, n0:n1], acc[t, h][:], IDENTITY, bias=bias_turned[:, t, 0:1])
             if t == 0:

@@ -1,3 +1,4 @@
+import math
 from contextlib import ExitStack
 
 import concourse.mybir as mybir
@@ -19,7 +20,8 @@ BLOCKS = M // P
 HALF = G // 2
 QUAD = 32
 SHARE = 88
-APART = 128 * 1024
+QUARTER = 64 * 1024
+WIDTH = {F32: 4, U32: 4, BF16: 2, U8: 1}
 
 FLOPS = 2 * D * M * G
 
@@ -34,50 +36,60 @@ def tile_attend_fill_bias_kernel(tc, xT, w, cache, bias, offs, slots, out):
     with ExitStack() as ctx:
         lists = ctx.enter_context(tc.tile_pool(name="lists", bufs=1))
         keep = ctx.enter_context(tc.tile_pool(name="keep", bufs=1))
-        ends = ctx.enter_context(tc.tile_pool(name="ends", bufs=1))
         psum = ctx.enter_context(tc.psum_pool(name="psum", bufs=1))
 
-        bias_rows = keep.tile([P, BLOCKS, QUAD], F32, name="bias_rows", align_bytes=64)
+        free = [q * QUARTER for q in range(4)]
+        placed = {}
+
+        def place(name, shape, dtype, quarter=None, over=None):
+            if over is None:
+                placed[name] = free[quarter]
+                free[quarter] = free[quarter] + math.prod(shape[1:]) * WIDTH[dtype]
+            else:
+                placed[name] = placed[over]
+            return keep.tile(shape, dtype, name=name, offset=placed[name], align_bytes=64)
+
+        bias_rows = place("bias_rows", [P, BLOCKS, QUAD], F32, 1)
         nc.vector.memset(bias_rows[:], 0.0)
 
         x_sb = {}
 
-        def load_x(g, j0, count):
-            rows = keep.tile([P, count, T], F32, name=f"x_{g}_{j0}")
+        def load_x(g, j0, count, quarter):
+            rows = place(f"x_{g}_{j0}", [P, count, T], F32, quarter)
             nc.sync.dma_start(out=rows[:], in_=x_rows[g, :, j0 : j0 + count, :])
             for j in range(count):
                 x_sb[g, j0 + j] = rows[:, j, :]
 
-        def load_w(g, m0, m1):
-            rows = keep.tile([P, PACK, m1 - m0], F32, name=f"w_{g}_{m0}", align_bytes=64)
+        def load_w(g, m0, m1, quarter):
+            rows = place(f"w_{g}_{m0}", [P, PACK, m1 - m0], F32, quarter)
             nc.sync.dma_start(out=rows[:], in_=w_rows[g, :, :, m0:m1])
             return rows
 
-        load_x(0, 0, 2)
+        load_x(0, 0, 2, 0)
         offs_sb = lists.tile([P, G // 16], U16, name="offs_sb")
         nc.sync.dma_start(offs_sb[:], offs)
         nc.sync.dma_start(out=bias_rows[0:P:QUAD], in_=bias.rearrange("(t q i) o -> q t (i o)", t=BLOCKS, i=QUAD))
-        load_x(0, 2, 2)
-        load_x(1, 0, 2)
-        load_x(1, 2, 1)
-        load_x(1, 3, 1)
-        w0_sb = load_w(0, 0, M)
+        load_x(0, 2, 2, 2)
+        load_x(1, 0, 2, 0)
+        load_x(1, 2, 1, 2)
+        load_x(1, 3, 1, 0)
+        w0_sb = load_w(0, 0, M, 2)
         w_sb = {(0, t): w0_sb[:, :, t * P : (t + 1) * P] for t in range(BLOCKS)}
         for t in range(BLOCKS):
-            w_sb[1, t] = load_w(1, t * P, (t + 1) * P)[:]
-        cache_sb = [ends.tile([P, T2], F32, name=f"cache_{t}", offset=t * APART) for t in range(BLOCKS)]
+            w_sb[1, t] = load_w(1, t * P, (t + 1) * P, 2 * t)[:]
+        cache_sb = [place(f"cache_{t}", [P, T2], F32, 2 * t) for t in range(BLOCKS)]
         nc.sync.dma_start(out=cache_sb[0][:], in_=cache_rows[0])
         slots_sb = lists.tile([P, G // 16], U16, name="slots_sb")
         nc.sync.dma_start(slots_sb[:], slots)
         nc.sync.dma_start(out=cache_sb[1][:], in_=cache_rows[1])
 
-        bias_turned = keep.tile([P, BLOCKS, QUAD], F32, name="bias_turned", align_bytes=64)
+        bias_turned = place("bias_turned", [P, BLOCKS, QUAD], F32, 1)
         for t in range(BLOCKS):
             nc.vector.transpose(bias_turned[:, t, :], bias_rows[:, t, :])
 
         def quantize(name, grouped, width):
-            codes = keep.tile([P, width], U32, name=f"{name}_codes", align_bytes=64)
-            scales = keep.tile([P, width], U8, name=f"{name}_scales", align_bytes=64)
+            codes = place(f"{name}_codes", [P, width], U32, 1)
+            scales = place(f"{name}_scales", [P, width], U8, 1)
             nc.vector.quantize_mx(
                 out=codes[:].bitcast(FP8X4),
                 scales=scales[:],
@@ -111,10 +123,10 @@ def tile_attend_fill_bias_kernel(tc, xT, w, cache, bias, offs, slots, out):
                 stop=(g == PASSES - 1),
             )
 
-        x_grouped = keep.tile([P, 2, PASSES, HALF, PACK], BF16, name="x_grouped", align_bytes=64)
+        x_grouped = place("x_grouped", [P, 2, PASSES, HALF, PACK], BF16, 3)
 
         def gather_pair(g, j0):
-            planes = keep.tile([P, 2, G], F32, name=f"planes_{g}_{j0}")
+            planes = place(f"planes_{g}_{j0}", [P, 2, G], F32, 1)
             for j in range(2):
                 nc.vector.tensor_copy(out=planes[:, j, :], in_=x_sb[g, j0 + j].indirect(offs_sb[:]))
             nc.scalar.copy(
@@ -136,7 +148,7 @@ def tile_attend_fill_bias_kernel(tc, xT, w, cache, bias, offs, slots, out):
             for g in range(PASSES):
                 x_mx[g, h] = (codes[:, g * HALF : (g + 1) * HALF], scales[:, g * HALF : (g + 1) * HALF])
 
-        first = [keep.tile([P, P, PACK], BF16, name=f"w{g}0_grouped", align_bytes=64) for g in range(PASSES)]
+        first = [place(f"w{g}0_grouped", [P, P, PACK], BF16, 3) for g in range(PASSES)]
         weave(nc.scalar, first[0][:], w_sb[0, 0])
         weave(nc.vector, first[1][:, 0:SHARE], w_sb[1, 0][:, :, 0:SHARE])
         weave(nc.scalar, first[1][:, SHARE:P], w_sb[1, 0][:, :, SHARE:P])
@@ -145,7 +157,7 @@ def tile_attend_fill_bias_kernel(tc, xT, w, cache, bias, offs, slots, out):
             for h in range(2):
                 multiply(g, 0, h, w_mx, x_mx[g, h])
 
-        second = keep.tile([P, PASSES, P, PACK], BF16, name="w_1_0", align_bytes=64)
+        second = place("w1_grouped", [P, PASSES, P, PACK], BF16, over="w_1_0")
         weave(nc.scalar, second[:, 0], w_sb[0, 1])
         weave(nc.vector, second[:, 1], w_sb[1, 1])
         for g in range(PASSES):
@@ -154,7 +166,7 @@ def tile_attend_fill_bias_kernel(tc, xT, w, cache, bias, offs, slots, out):
                 multiply(g, 1, h, w_mx, x_mx[g, h])
 
         for t in range(BLOCKS):
-            y = ends.tile([P, G], F32, name=f"y_{t}", offset=t * APART + 4 * T2)
+            y = place(f"y_{t}", [P, G], F32, 2 * t + 1)
             for h, (n0, n1) in enumerate(halves):
                 nc.scalar.activation(y[:, n0:n1], acc[t, h][:], IDENTITY, bias=bias_turned[:, t, 0:1])
             if t == 0:

@@ -21,6 +21,7 @@ HALF = G // 2
 QUAD = 32
 SHARE = 88
 QUARTER = 64 * 1024
+BURST = 256
 WIDTH = {F32: 4, U32: 4, BF16: 2, U8: 1}
 
 FLOPS = 2 * D * M * G
@@ -44,10 +45,10 @@ def tile_attend_fill_bias_kernel(tc, xT, w, cache, bias, offs, slots, out):
         def place(name, shape, dtype, quarter=None, over=None):
             if over is None:
                 placed[name] = free[quarter]
-                free[quarter] = free[quarter] + math.prod(shape[1:]) * WIDTH[dtype]
+                free[quarter] = free[quarter] + math.ceil(math.prod(shape[1:]) * WIDTH[dtype] / BURST) * BURST
             else:
                 placed[name] = placed[over]
-            return keep.tile(shape, dtype, name=name, offset=placed[name], align_bytes=64)
+            return keep.tile(shape, dtype, name=name, offset=placed[name], align_bytes=BURST)
 
         bias_rows = place("bias_rows", [P, BLOCKS, QUAD], F32, 1)
         nc.vector.memset(bias_rows[:], 0.0)

@@ -19,9 +19,8 @@ PASSES = D // (P * PACK)
 BLOCKS = M // P
 HALF = G // 2
 QUAD = 32
-SHARE = 88
 QUARTER = 64 * 1024
-BURST = 256
+BURST = 512
 WIDTH = {F32: 4, U32: 4, BF16: 2, U8: 1}
 
 FLOPS = 2 * D * M * G
@@ -66,18 +65,16 @@ def tile_attend_fill_bias_kernel(tc, xT, w, cache, bias, offs, slots, out):
             nc.sync.dma_start(out=rows[:], in_=w_rows[g, :, :, m0:m1])
             return rows
 
-        load_x(0, 0, 2, 0)
+        load_x(0, 0, 4, 0)
         offs_sb = lists.tile([P, G // 16], U16, name="offs_sb")
         nc.sync.dma_start(offs_sb[:], offs)
         nc.sync.dma_start(out=bias_rows[0:P:QUAD], in_=bias.rearrange("(t q i) o -> q t (i o)", t=BLOCKS, i=QUAD))
-        load_x(0, 2, 2, 2)
-        load_x(1, 0, 2, 0)
-        load_x(1, 2, 1, 2)
-        load_x(1, 3, 1, 0)
-        w0_sb = load_w(0, 0, M, 2)
-        w_sb = {(0, t): w0_sb[:, :, t * P : (t + 1) * P] for t in range(BLOCKS)}
-        for t in range(BLOCKS):
-            w_sb[1, t] = load_w(1, t * P, (t + 1) * P, 2 * t)[:]
+        load_x(1, 0, 2, 2)
+        load_x(1, 2, 1, 0)
+        load_x(1, 3, 1, 2)
+        w_sb = {
+            (g, t): load_w(g, t * P, (t + 1) * P, 2 * g)[:] for t in range(BLOCKS) for g in range(PASSES)
+        }
         cache_sb = [place(f"cache_{t}", [P, T2], F32, 2 * t) for t in range(BLOCKS)]
         nc.sync.dma_start(out=cache_sb[0][:], in_=cache_rows[0])
         slots_sb = lists.tile([P, G // 16], U16, name="slots_sb")
@@ -106,6 +103,13 @@ def tile_attend_fill_bias_kernel(tc, xT, w, cache, bias, offs, slots, out):
             else:
                 nc.scalar.activation(target, source, COPY)
 
+        def gather(engine, plane, window, n0=0, n1=G):
+            picked = window.indirect(offs_sb[:, n0 // 16 : n1 // 16])
+            if engine is nc.vector:
+                nc.vector.tensor_copy(out=plane, in_=picked)
+            else:
+                nc.scalar.activation(plane, picked, COPY)
+
         halves = [(0, G // 2), (G // 2, G)]
         acc = {
             (t, h): psum.tile([P, G // 2], F32, name=f"acc_{t}_{h}")
@@ -124,47 +128,27 @@ def tile_attend_fill_bias_kernel(tc, xT, w, cache, bias, offs, slots, out):
                 stop=(g == PASSES - 1),
             )
 
-        x_grouped = place("x_grouped", [P, 2, PASSES, HALF, PACK], BF16, 3)
-
-        def gather_pair(g, j0):
-            planes = place(f"planes_{g}_{j0}", [P, 2, G], F32, 1)
-            for j in range(2):
-                nc.vector.tensor_copy(out=planes[:, j, :], in_=x_sb[g, j0 + j].indirect(offs_sb[:]))
-            nc.scalar.copy(
-                x_grouped[:, :, g, :, j0 : j0 + 2].rearrange("p h (c i) j -> p h c j i", i=4),
-                planes[:].rearrange("p j (h c i) -> p h c j i", h=2, i=4),
-            )
-
-        gather_pair(0, 0)
-        gather_pair(0, 2)
-        gather_pair(1, 0)
-        nc.vector.tensor_copy(out=x_grouped[:, :, 1, :, 2], in_=x_sb[1, 2].indirect(offs_sb[:]))
-        for h, (n0, n1) in enumerate(halves):
-            nc.vector.tensor_copy(
-                out=x_grouped[:, h, 1, :, 3], in_=x_sb[1, 3].indirect(offs_sb[:, n0 // 16 : n1 // 16])
-            )
         x_mx = {}
-        for h in range(2):
-            codes, scales = quantize(f"x{h}", x_grouped[:, h].rearrange("p g n j -> p (g n) j"), PASSES * HALF)
+        for g in range(PASSES):
+            pair = place(f"pair_{g}", [P, 2, G], F32, 1)
+            for j in range(2):
+                gather(nc.scalar if g else nc.vector, pair[:, j, :], x_sb[g, j])
+            grouped = place(f"x_grouped_{g}", [P, G, PACK], BF16, 3)
+            weave(nc.scalar, grouped[:, :, 0:2], pair[:])
+            for j in range(2, PACK):
+                gather(nc.vector, grouped[:, :, j], x_sb[g, j])
+            codes, scales = quantize(f"x{g}", grouped[:], G)
+            for h, (n0, n1) in enumerate(halves):
+                x_mx[g, h] = (codes[:, n0:n1], scales[:, n0:n1])
+
+        for t in range(BLOCKS):
+            woven = [place(f"w{g}{t}_grouped", [P, P, PACK], BF16, 3) for g in range(PASSES)]
             for g in range(PASSES):
-                x_mx[g, h] = (codes[:, g * HALF : (g + 1) * HALF], scales[:, g * HALF : (g + 1) * HALF])
-
-        first = [place(f"w{g}0_grouped", [P, P, PACK], BF16, 3) for g in range(PASSES)]
-        weave(nc.scalar, first[0][:], w_sb[0, 0])
-        weave(nc.vector, first[1][:, 0:SHARE], w_sb[1, 0][:, :, 0:SHARE])
-        weave(nc.scalar, first[1][:, SHARE:P], w_sb[1, 0][:, :, SHARE:P])
-        for g in range(PASSES):
-            w_mx = quantize(f"w{g}0", first[g][:], P)
-            for h in range(2):
-                multiply(g, 0, h, w_mx, x_mx[g, h])
-
-        second = place("w1_grouped", [P, PASSES, P, PACK], BF16, over="w_1_0")
-        weave(nc.scalar, second[:, 0], w_sb[0, 1])
-        weave(nc.vector, second[:, 1], w_sb[1, 1])
-        for g in range(PASSES):
-            w_mx = quantize(f"w{g}1", second[:, g], P)
-            for h in range(2):
-                multiply(g, 1, h, w_mx, x_mx[g, h])
+                weave(nc.vector if g == t == 1 else nc.scalar, woven[g][:], w_sb[g, t])
+            for g in range(PASSES):
+                w_mx = quantize(f"w{g}{t}", woven[g][:], P)
+                for h in range(2):
+                    multiply(g, t, h, w_mx, x_mx[g, h])
 
         for t in range(BLOCKS):
             y = place(f"y_{t}", [P, G], F32, 2 * t + 1)

@@ -21,6 +21,7 @@ HALF = G // 2
 QUAD = 32
 QUARTER = 64 * 1024
 BURST = 512
+PAGE = 4096
 WIDTH = {F32: 4, U32: 4, BF16: 2, U8: 1}
 
 FLOPS = 2 * D * M * G
@@ -39,15 +40,13 @@ def tile_attend_fill_bias_kernel(tc, xT, w, cache, bias, offs, slots, out):
         psum = ctx.enter_context(tc.psum_pool(name="psum", bufs=1))
 
         free = [q * QUARTER for q in range(4)]
-        placed = {}
 
-        def place(name, shape, dtype, quarter=None, over=None):
-            if over is None:
-                placed[name] = free[quarter]
-                free[quarter] = free[quarter] + math.ceil(math.prod(shape[1:]) * WIDTH[dtype] / BURST) * BURST
-            else:
-                placed[name] = placed[over]
-            return keep.tile(shape, dtype, name=name, offset=placed[name], align_bytes=BURST)
+        def place(name, shape, dtype, quarter):
+            size = math.prod(shape[1:]) * WIDTH[dtype]
+            boundary = PAGE if size >= PAGE else BURST
+            offset = math.ceil(free[quarter] / boundary) * boundary
+            free[quarter] = offset + size
+            return keep.tile(shape, dtype, name=name, offset=offset, align_bytes=boundary)
 
         bias_rows = place("bias_rows", [P, BLOCKS, QUAD], F32, 1)
         nc.vector.memset(bias_rows[:], 0.0)

@@ -53,9 +53,9 @@ def tile_attend_fill_bias_kernel(tc, xT, w, cache, bias, offs, slots, out):
 
         x_sb = {}
 
-        def load_x(g, j0, count, quarter):
+        def load_x(g, j0, count, quarter, queue=nc.sync):
             rows = place(f"x_{g}_{j0}", [P, count, T], F32, quarter)
-            nc.sync.dma_start(out=rows[:], in_=x_rows[g, :, j0 : j0 + count, :])
+            queue.dma_start(out=rows[:], in_=x_rows[g, :, j0 : j0 + count, :])
             for j in range(count):
                 x_sb[g, j0 + j] = rows[:, j, :]
 
@@ -64,10 +64,13 @@ def tile_attend_fill_bias_kernel(tc, xT, w, cache, bias, offs, slots, out):
             nc.sync.dma_start(out=rows[:], in_=w_rows[g, :, :, m0:m1])
             return rows
 
-        load_x(0, 0, 4, 0)
+        load_x(0, 0, 2, 0, nc.scalar)
         offs_sb = lists.tile([P, G // 16], U16, name="offs_sb")
         nc.sync.dma_start(offs_sb[:], offs)
+        slots_sb = lists.tile([P, G // 16], U16, name="slots_sb")
+        nc.sync.dma_start(slots_sb[:], slots)
         nc.sync.dma_start(out=bias_rows[0:P:QUAD], in_=bias.rearrange("(t q i) o -> q t (i o)", t=BLOCKS, i=QUAD))
+        load_x(0, 2, 2, 0)
         load_x(1, 0, 2, 2)
         load_x(1, 2, 1, 0)
         load_x(1, 3, 1, 2)
@@ -76,8 +79,6 @@ def tile_attend_fill_bias_kernel(tc, xT, w, cache, bias, offs, slots, out):
         }
         cache_sb = [place(f"cache_{t}", [P, T2], F32, 2 * t) for t in range(BLOCKS)]
         nc.sync.dma_start(out=cache_sb[0][:], in_=cache_rows[0])
-        slots_sb = lists.tile([P, G // 16], U16, name="slots_sb")
-        nc.sync.dma_start(slots_sb[:], slots)
         nc.sync.dma_start(out=cache_sb[1][:], in_=cache_rows[1])
 
         bias_turned = place("bias_turned", [P, BLOCKS, QUAD], F32, 1)

@@ -64,13 +64,13 @@ def tile_attend_fill_bias_kernel(tc, xT, w, cache, bias, offs, slots, out):
             nc.sync.dma_start(out=rows[:], in_=w_rows[g, :, :, m0:m1])
             return rows
 
+        load_x(0, 2, 2, 0)
         load_x(0, 0, 2, 0, nc.scalar)
         offs_sb = lists.tile([P, G // 16], U16, name="offs_sb")
         nc.sync.dma_start(offs_sb[:], offs)
         slots_sb = lists.tile([P, G // 16], U16, name="slots_sb")
         nc.sync.dma_start(slots_sb[:], slots)
         nc.sync.dma_start(out=bias_rows[0:P:QUAD], in_=bias.rearrange("(t q i) o -> q t (i o)", t=BLOCKS, i=QUAD))
-        load_x(0, 2, 2, 0)
         load_x(1, 0, 2, 2)
         load_x(1, 2, 1, 0)
         load_x(1, 3, 1, 2)

import math
from contextlib import ExitStack

import concourse.mybir as mybir

F32 = mybir.dt.float32
BF16 = mybir.dt.bfloat16
U32 = mybir.dt.uint32
U16 = mybir.dt.uint16
U8 = mybir.dt.uint8
FP8X4 = mybir.dt.float8_e4m3fn_x4
COPY = mybir.ActivationFunctionType.Copy
IDENTITY = mybir.ActivationFunctionType.Identity

P = 128
PACK = 4
G, T, T2, D, M = 256, 1024, 1024, 1024, 256
PASSES = D // (P * PACK)
BLOCKS = M // P
HALF = G // 2
QUAD = 32
QUARTER = 64 * 1024
BURST = 512
PAGE = 4096
WIDTH = {F32: 4, U32: 4, BF16: 2, U8: 1}

FLOPS = 2 * D * M * G


def tile_attend_fill_bias_kernel(tc, xT, w, cache, bias, offs, slots, out):
    nc = tc.nc
    x_rows = xT.rearrange("(g p j) n -> g p j n", p=P, j=PACK)
    w_rows = w.rearrange("(g p j) m -> g p j m", p=P, j=PACK)
    cache_rows = cache.rearrange("(t p) n -> t p n", p=P)
    out_rows = out.rearrange("(t p) n -> t p n", p=P)

    with ExitStack() as ctx:
        lists = ctx.enter_context(tc.tile_pool(name="lists", bufs=1))
        keep = ctx.enter_context(tc.tile_pool(name="keep", bufs=1))
        psum = ctx.enter_context(tc.psum_pool(name="psum", bufs=1))

        free = [q * QUARTER for q in range(4)]

        def place(name, shape, dtype, quarter):
            size = math.prod(shape[1:]) * WIDTH[dtype]
            boundary = PAGE if size >= PAGE else BURST
            offset = math.ceil(free[quarter] / boundary) * boundary
            free[quarter] = offset + size
            return keep.tile(shape, dtype, name=name, offset=offset, align_bytes=boundary)

        bias_rows = place("bias_rows", [P, BLOCKS, QUAD], F32, 1)
        nc.vector.memset(bias_rows[:], 0.0)

        x_sb = {}

        def load_x(g, j0, count, quarter, queue=nc.sync):
            rows = place(f"x_{g}_{j0}", [P, count, T], F32, quarter)
            queue.dma_start(out=rows[:], in_=x_rows[g, :, j0 : j0 + count, :])
            for j in range(count):
                x_sb[g, j0 + j] = rows[:, j, :]

        def load_w(g, m0, m1, quarter):
            rows = place(f"w_{g}_{m0}", [P, PACK, m1 - m0], F32, quarter)
            nc.sync.dma_start(out=rows[:], in_=w_rows[g, :, :, m0:m1])
            return rows

        load_x(0, 2, 2, 0)
        load_x(0, 0, 2, 0, nc.scalar)
        offs_sb = lists.tile([P, G // 16], U16, name="offs_sb")
        nc.sync.dma_start(offs_sb[:], offs)
        slots_sb = lists.tile([P, G // 16], U16, name="slots_sb")
        nc.sync.dma_start(slots_sb[:], slots)
        nc.sync.dma_start(out=bias_rows[0:P:QUAD], in_=bias.rearrange("(t q i) o -> q t (i o)", t=BLOCKS, i=QUAD))
        load_x(1, 0, 2, 2)
        load_x(1, 2, 1, 0)
        load_x(1, 3, 1, 2)
        w_sb = {
            (g, t): load_w(g, t * P, (t + 1) * P, 2 * g)[:] for t in range(BLOCKS) for g in range(PASSES)
        }
        cache_sb = [place(f"cache_{t}", [P, T2], F32, 2 * t) for t in range(BLOCKS)]
        nc.sync.dma_start(out=cache_sb[0][:], in_=cache_rows[0])
        nc.sync.dma_start(out=cache_sb[1][:], in_=cache_rows[1])

        bias_turned = place("bias_turned", [P, BLOCKS, QUAD], F32, 1)
        for t in range(BLOCKS):
            nc.vector.transpose(bias_turned[:, t, :], bias_rows[:, t, :])

        def quantize(name, grouped, width):
            codes = place(f"{name}_codes", [P, width], U32, 1)
            scales = place(f"{name}_scales", [P, width], U8, 1)
            nc.vector.quantize_mx(
                out=codes[:].bitcast(FP8X4),
                scales=scales[:],
                in_=grouped.rearrange("p n j -> p (n j)"),
            )
            return codes[:], scales[:]

        def weave(engine, grouped, rows):
            target = grouped.rearrange("p (c i) j -> p c j i", i=4)
            source = rows.rearrange("p j (c i) -> p c j i", i=4)
            if engine is nc.vector:
                nc.vector.tensor_copy(out=target, in_=source)
            else:
                nc.scalar.activation(target, source, COPY)

        def gather(engine, plane, window, n0=0, n1=G):
            picked = window.indirect(offs_sb[:, n0 // 16 : n1 // 16])
            if engine is nc.vector:
                nc.vector.tensor_copy(out=plane, in_=picked)
            else:
                nc.scalar.activation(plane, picked, COPY)

        halves = [(0, G // 2), (G // 2, G)]
        acc = {
            (t, h): psum.tile([P, G // 2], F32, name=f"acc_{t}_{h}")
            for t in range(BLOCKS)
            for h in range(2)
        }

        def multiply(g, t, h, w_mx, x_mx):
            nc.tensor.matmul_mx(
                out=acc[t, h][:],
                lhsT=w_mx[0].bitcast(FP8X4),
                lhsT_scale=w_mx[1],
                rhs=x_mx[0].bitcast(FP8X4),
                rhs_scale=x_mx[1],
                start=(g == 0),
                stop=(g == PASSES - 1),
            )

        x_mx = {}
        for g in range(PASSES):
            pair = place(f"pair_{g}", [P, 2, G], F32, 1)
            for j in range(2):
                gather(nc.scalar if g else nc.vector, pair[:, j, :], x_sb[g, j])
            grouped = place(f"x_grouped_{g}", [P, G, PACK], BF16, 3)
            weave(nc.scalar, grouped[:, :, 0:2], pair[:])
            for j in range(2, PACK):
                gather(nc.vector, grouped[:, :, j], x_sb[g, j])
            codes, scales = quantize(f"x{g}", grouped[:], G)
            for h, (n0, n1) in enumerate(halves):
                x_mx[g, h] = (codes[:, n0:n1], scales[:, n0:n1])

        for t in range(BLOCKS):
            woven = [place(f"w{g}{t}_grouped", [P, P, PACK], BF16, 3) for g in range(PASSES)]
            for g in range(PASSES):
                weave(nc.vector if g == t == 1 else nc.scalar, woven[g][:], w_sb[g, t])
            for g in range(PASSES):
                w_mx = quantize(f"w{g}{t}", woven[g][:], P)
                for h in range(2):
                    multiply(g, t, h, w_mx, x_mx[g, h])

        for t in range(BLOCKS):
            y = place(f"y_{t}", [P, G], F32, 2 * t + 1)
            for h, (n0, n1) in enumerate(halves):
                nc.scalar.activation(y[:, n0:n1], acc[t, h][:], IDENTITY, bias=bias_turned[:, t, 0:1])
            if t == 0:
                nc.vector.tensor_copy(out=cache_sb[t][:].indirect(slots_sb[:]), in_=y[:])
            else:
                nc.scalar.activation(cache_sb[t][:].indirect(slots_sb[:]), y[:], COPY)
            nc.sync.dma_start(out=out_rows[t], in_=cache_sb[t][:])
